import numpy as np, ml_dtypes
CORES = [8,136,40,168]
N = 4
BF = ml_dtypes.bfloat16
def gentries(a):
    return np.ascontiguousarray(a.reshape(8, 16, -1).transpose(0, 2, 1)).reshape(8, -1)
def gtable(e):
    e = np.asarray(e); return np.ascontiguousarray(e.reshape(8, -1, 16).transpose(0, 2, 1)).reshape(128, -1).astype(np.int32)
W, K, F, O, C, V = 2048, 480, 1, 8, 16, 250
def pick(a, ix):
    return np.take_along_axis(a, ix[:, None, :], 2)
def draw_lists(rng):
    return rng.permuted(np.tile(np.arange(W, dtype=np.int64), (N, 8, N, F, O, 1)), axis=-1)[..., :K].copy()
def frames(rng, T, L, share):
    o = rng.integers(0, O, (N, 8, N, F)); B = np.zeros((N, 8, 16, N, F, K), np.int64)
    for r in range(N):
        for q in range(N):
            for f in range(F):
                v = pick(T[q], L[r, np.arange(8), q, f, o[r, :, q, f]]) + rng.integers(-10, 11, (8, 16, K))
                m = rng.random((8, 16, K)) < share[r, :, q, f][:, None, None]
                B[r, :, :, q, f] = np.clip(np.where(m, v, rng.integers(-V, V + 1, (8, 16, K))), -V, V)
    return B
def pack(R, B, L):
    return {"ref0": np.ascontiguousarray(R.reshape(N, 128, W)).astype(np.float32).astype(BF), "obs": np.ascontiguousarray(B.reshape(N, 128, N * F * K)).astype(np.float32).astype(BF),
            "ops": np.stack([gtable(a.reshape(8, -1)) for a in L])}
def setup_inputs(rng):
    T = rng.integers(-200, 201, (N, 8, 16, W)); R = T + rng.integers(-40, 41, T.shape); L = draw_lists(rng)
    share = rng.choice(np.array([1.0, 0.3, 0.02, 0.0]), (N, 8, N, F))
    return pack(R, frames(rng, T, L, share), L)
def setup_inputs_chain(rng):
    R = rng.integers(-200, 201, (N, 8, 16, W)); L = draw_lists(rng); B = np.zeros((N, 8, 16, N, F, K), np.int64)
    for q in range(N):
        for g in range(8):
            c = rng.permutation(W); P, Q = c[:K], c[K:2 * K]; R[q, g][:, Q] = R[q, g][:, P]
            away = rng.integers(1, 51, (16, K)) * (2 * rng.integers(0, 2, (16, K)) - 1)
            for r in range(N):
                for f in range(F):
                    z = rng.permutation(K); o = rng.permutation(O); e = 1 if rng.random() < 0.7 else -1
                    L[r, g, q, f, o[0]] = P[z]; L[r, g, q, f, o[1]] = Q[z]
                    B[r, g, :, q, f] = (R[q, g][:, P] + e * away)[:, z]
    return pack(R, B, L)
def setup_inputs_edges(rng):
    R = rng.integers(-200, 201, (N, 8, 16, W)); L = draw_lists(rng); B = np.zeros((N, 8, 16, N, F, K), np.int64)
    o = rng.integers(0, O, (N, 8, N, F)); same = rng.random((N, 8, N, F)) < 0.3
    for q in range(N):
        same[q, 0, q, 0] = True; same[q, 1, q, 0] = False
        for r in range(N):
            for f in range(F):
                s = rng.choice(np.array([0, 1, C - 1, C, C + 1, 2 * C]), (8, 16, K)) * (2 * rng.integers(0, 2, (8, 16, K)) - 1)
                B[r, :, :, q, f] = pick(R[q], L[r, np.arange(8), q, f, o[r, :, q, f]]) + np.where(same[r, :, q, f][:, None, None], 0, s)
    return pack(R, B, L)
def setup_inputs_ends(rng):
    R = rng.integers(10, V + 1, (N, 8, 16, W)); L = draw_lists(rng); B = rng.choice(np.array([-V, 1 - V, -1, 0, 1, V - 1, V]), (N, 8, 16, N, F, K))
    runs = [np.arange(K), np.arange(W - K, W), np.arange(K)[::-1], np.arange(W - 1, W - 1 - K, -1), np.arange(K) * (W // K)]
    z = rng.permuted(np.tile(np.arange(8), (N, 1)), axis=1)
    for q in range(N):
        for g in range(8):
            s = 2 * int(rng.integers(0, 2)) - 1; k = int(z[q, g])
            for r in range(N):
                for f in range(F):
                    for o in range(O):
                        i = int(rng.integers(0, len(runs) + 1))
                        L[r, g, q, f, o] = runs[i] if i < len(runs) else np.concatenate([[W - 1], 1 + rng.permutation(W - 2)[:K - 2], [0]])
            if k < 4: R[q, g] = rng.integers(V - 1 if k < 2 else 200, V + 1, (16, W))
            c = rng.permutation(W)
            for t in range(N * F if k % 2 == 1 else 1):
                r, f = (q + t // F) % N, t % F; p1, p2 = c[K - 1 + 2 * t], c[K + 2 * t]
                i = int(rng.integers(0, 16)); a = 259 + (k // 2) % 2 + 4 * int(rng.integers(0, 59)) - V
                R[q, g][:, p2] = R[q, g][:, p1]; R[q, g, i, p1] = a; R[q, g, i, p2] = a + 1
                near = np.append(c[:K - 1], p1); far = np.append(c[:K - 1], p2)
                w = int(rng.integers(1, O))
                if k == 0:
                    w = 1 + 3 * int(rng.integers(0, (O + 1) // 3))
                    if int(np.sum(R[q, g][:, near] + V)) % 2 == 1: R[q, g, 0, c[0]] = 2 * V - 1 - R[q, g, 0, c[0]]
                if k in (2, 3): w = 1 + 2 * int(rng.integers(0, O // 2))
                B[r, g, :, q, f] = -s * V
                for o in range(O): L[r, g, q, f, o] = rng.permutation(near if o == w else far)
            R[q, g] = s * R[q, g]
    return pack(R, B, L)
def setup_inputs_ties(rng):
    s = 2 * rng.integers(0, 2, (N, 8, 16, 1)) - 1; m = rng.integers(N * F * C - V, V - 2 * C, (N, 8, 16, 1))
    R = m + rng.integers(C, 2 * C + 1, (N, 8, 16, W)); R[..., W - 1] = V
    L = np.zeros((N, 8, N, F, O, K), np.int64); B = np.zeros((N, 8, 16, N, F, K), np.int64)
    for q in range(N):
        for g in range(8):
            S = rng.permutation(W - 1)[:K]
            for t in range(N * F):
                r, f = (q + t // F) % N, t % F
                if rng.random() < 0.5: S = rng.permutation(W - 1)[:K]
                w = int(rng.integers(0, O))
                for o in range(O):
                    p = rng.permutation(S)
                    if o < w or (o > w and rng.random() < 0.5): p[rng.integers(0, K)] = W - 1
                    L[r, g, q, f, o] = p
                B[r, g, :, q, f] = s[q, g] * (m[q, g] - t * C + rng.integers(0, C + 1, (16, K)))
    return pack(R * s, B, L)
def setup_inputs_spread(rng):
    z = np.exp2(-rng.integers(0, 9, (N, 8, 1, W)).astype(np.float64))
    T = (rng.integers(-V, V + 1, (N, 8, 16, W)) * z).astype(np.int64); R = np.clip(T + (rng.integers(-60, 61, T.shape) * z).astype(np.int64), -V, V); L = draw_lists(rng)
    share = rng.choice(np.array([1.0, 0.6, 0.1, 0.02, 0.0]), (N, 8, N, F))
    return pack(R, frames(rng, T, L, share), L)
def check_inputs(d):
    bad = []
    for k in ("ref0", "obs"):
        v = np.asarray(d[k]).astype(np.float32)
        if not (np.all(np.abs(v) <= V) and np.all(v == np.rint(v))): bad.append("range of " + k)
    if np.min(d["ops"]) < 0 or np.max(d["ops"]) > W - 1: bad.append("range of ops")
    for a in d["ops"]:
        e = np.sort(gentries(a).reshape(8, -1, K), axis=-1)
        if np.any(e[..., 1:] == e[..., :-1]):
            bad.append("repeated number in a list of ops"); break
    return bad
def reference(ref0, obs, ops):
    R = ref0.astype(np.float32).astype(np.int32).reshape(N, 8, 16, W); x = obs.astype(np.float32).astype(np.int32).reshape(N, 8, 16, N, F, K)
    L = np.stack([gentries(a) for a in ops]).astype(np.int64).reshape(N, 8, N, F, O, K)
    g, i = np.arange(8)[:, None, None], np.arange(16)[None, :, None]
    for q in range(N):
        for d in range(N):
            r = (q + d) % N
            for f in range(F):
                b = x[r, :, :, q, f]
                cost = np.stack([np.sum(np.abs(b - pick(R[q], L[r, :, q, f, o])), axis=(1, 2)) for o in range(O)])
                win = np.argmin(cost, axis=0)
                ix = L[r, np.arange(8), q, f, win]
                v = pick(R[q], ix)
                R[q][g, i, ix[:, None, :]] = v + np.clip(b - v, -C, C)
    return {"y": R.reshape(N, 128, W).astype(np.float32).astype(BF)}

@@ -1,0 +1,205 @@
+from concourse.mybir import AluOpType, AxisListType, ActivationFunctionType
+
+N, W, K, O, C = 4, 2048, 480, 8, 16
+KC = K // 16
+LC = O * KC
+CA = 12
+KA = 16 * CA
+CENTRE = -float(15 * 2 ** 20)
+
+SCRATCH = {
+    "win": ("sbuf", [128, W], "bfloat16"),
+    "l32": ("sbuf", [128, N * LC], "int32"),
+    "bb": ("sbuf", [128, N * K], "bfloat16"),
+    "sl": ("sbuf", [128, (N - 1) * LC], "int32"),
+    "sb": ("sbuf", [128, (N - 1) * K], "bfloat16"),
+    "l16": ("sbuf", [128, N * LC], "uint16"),
+    "rs": ("sbuf", [128, O * K], "bfloat16"),
+    "junk": ("sbuf", [128, 4 * K], "float32"),
+    "acc": ("sbuf", [128, O], "float32"),
+    "mm": ("sbuf", [128, 2], "float32"),
+    "w30": ("sbuf", [128, 1], "float32"),
+    "off": ("sbuf", [128, 2], "uint16"),
+    "ofr": ("sbuf", [128, KC], "uint16"),
+    "lw": ("sbuf", [128, 32], "uint16"),
+    "rw": ("sbuf", [128, K], "bfloat16"),
+    "cl": ("sbuf", [128, K], "bfloat16"),
+    "ones": ("sbuf", [128, 128], "bfloat16"),
+    "eights": ("sbuf", [128, 128], "float32"),
+    "gt": ("sbuf", [128, 128], "float32"),
+    "g8": ("sbuf", [128, 128], "float32"),
+    "idp": ("sbuf", [128, 128], "bfloat16"),
+    "idn": ("sbuf", [128, 128], "bfloat16"),
+    "cen": ("sbuf", [128, O], "bfloat16"),
+    "ov": ("sbuf", [128, O], "bfloat16"),
+    "pi": ("sbuf", [128, 1], "int32"),
+    "pq": ("sbuf", [128, 1], "int32"),
+    "pf": ("sbuf", [128, 1], "float32"),
+    "jt": ("sbuf", [128, KC], "float32"),
+    "jc": ("sbuf", [128, 2], "float32"),
+    "jr": ("sbuf", [128, KC], "float32"),
+}
+for _k in range(O):
+    SCRATCH["pw%d" % _k] = ("psum", [128, 512], "float32")
+SEMAPHORES = ["ref", "l0", "b0", "l1", "b1", "rest", "sent", "stored",
+              "al1", "al2", "al3", "ab1", "ab2", "ab3",
+              "fill", "gio", "gid", "gg1", "gg2", "c1", "c2", "cst",
+              "cv", "sc", "vg0", "vg1", "sg0", "sg1", "pe0", "pe1", "pe2", "pe3", "pe4", "pe5", "pe6", "pe7",
+              "vr0", "vr", "sa0", "sa",
+              "k1", "k2", "m12", "t1", "t2", "t3", "lg", "ra", "rb", "pa", "pb", "cl"]
+
+
+def rank_program(g, core, T, topo):
+    rank = T.rank_of(core)
+    if rank is None:
+        return
+    S = T.sem
+    V, A, P, Y = g.vector, g.scalar, g.tensor, g.sync
+    op, fn = AluOpType, ActivationFunctionType
+    X = AxisListType.X
+    pw = [T["pw%d" % k] for k in range(O)]
+    pk1, pk2, pta, ptb = pw[0], pw[4], pw[1], pw[5]
+
+    Y.dma_start(T.l32[:, 0:LC], T.ops[:, rank * LC:(rank + 1) * LC]).then_inc(S.l0, 16)
+    Y.dma_start(T.win[:], T.ref0[:]).then_inc(S.ref, 16)
+    Y.dma_start(T.bb[:, 0:K], T.obs[:, rank * K:(rank + 1) * K]).then_inc(S.b0, 16)
+    for d in range(1, N):
+        q = (rank - d) % N
+        Y.dma_start(T.sl[:, (d - 1) * LC:d * LC], T.ops[:, q * LC:(q + 1) * LC]).then_inc(S.l1 if d == 1 else S.rest, 16)
+        Y.dma_start(T.sb[:, (d - 1) * K:d * K], T.obs[:, q * K:(q + 1) * K]).then_inc(S.b1 if d == 1 else S.rest, 16)
+
+    V.memset(T.ones[:], 1.0).then_inc(S.fill, 1)
+    V.memset(T.eights[:], 8.0).then_inc(S.fill, 1)
+    V.memset(T.cen[:], CENTRE).then_inc(S.fill, 1)
+    g.iota(T.pi[:], [[0, 1]], 0, 1).then_inc(S.gio, 1)
+    g.iota(T.jt[:], [[16, KC]], 0, 1, allow_small_or_imprecise_dtypes=True).then_inc(S.gio, 1)
+    g.iota(T.ov[:], [[1, O]], 0, 0, allow_small_or_imprecise_dtypes=True).then_inc(S.gio, 1)
+    g.wait_ge(S.fill, 3)
+    g.affine_select(T.idp[:], T.ones[:], [[-1, 128]], op.is_equal, 0.0, 0, 1).then_inc(S.gid, 1)
+    g.affine_select(T.gt[:], T.eights[:], [[-16, 8], [0, 16]], op.is_ge, 0.0, 0, 1).then_inc(S.gg1, 1)
+    g.wait_ge(S.gg1, 1)
+    g.affine_select(T.g8[:], T.gt[:], [[16, 8], [0, 16]], op.is_ge, 0.0, 15, -1).then_inc(S.gg2, 1)
+    V.wait_ge(S.gio, 3)
+    V.tensor_scalar(T.pq[:], T.pi[:], 112, None, op.bitwise_and).then_inc(S.c1, 1)
+    V.wait_ge(S.c1, 1)
+    V.tensor_copy(T.pf[:], T.pq[:]).then_inc(S.c2, 1)
+    V.wait_ge(S.c2, 1)
+    V.tensor_scalar(T.jc[:], T.jt[:, 0:2], T.pf[:], float(KC - 1), op.subtract, op.min).then_inc(S.cst, 1)
+    V.tensor_scalar(T.jr[:], T.jt[:], T.pf[:], 1.0 / 16, op.subtract, op.mult).then_inc(S.cst, 1)
+    V.wait_ge(S.gid, 1)
+    V.tensor_scalar(T.idn[:], T.idp[:], -1.0, None, op.mult).then_inc(S.cst, 1)
+    V.wait_ge(S.cst, 3)
+    P.wait_ge(S.cst, 3)
+    P.wait_ge(S.gg2, 1)
+
+    sent = 0
+    arrive = {}
+    for d in range(1, N):
+        dst = T.cores[(rank - d) % N]
+        rid, pid = topo.addr(dst, core)
+        m = topo.mask(core, dst)
+        if d == 1:
+            g.wait_ge(S.l1, 16)
+        if d == 2:
+            g.wait_ge(S.rest, 16 * 2 * (N - 2))
+        g.remote_dma(T.l32[:, d * LC:(d + 1) * LC], T.sl[:, (d - 1) * LC:d * LC], S["al%d" % d], S.sent, pid, rid, m)
+        if d == 1:
+            g.wait_ge(S.b1, 16)
+        g.remote_dma(T.bb[:, d * K:(d + 1) * K], T.sb[:, (d - 1) * K:d * K], S["ab%d" % d], S.sent, pid, rid, m)
+        sent += 2 * len(topo.engines(core, dst))
+        arrive[d] = len(topo.engines(T.cores[(rank + d) % N], core))
+    g.wait_ge(S.sent, sent)
+
+    ncv = [0]
+
+    def convert(d):
+        V.tensor_copy(T.l16[:, d * LC:(d + 1) * LC], T.l32[:, d * LC:(d + 1) * LC]).then_inc(S.cv, 1)
+        ncv[0] += 1
+
+    V.wait_ge(S.l0, 16)
+    convert(0)
+
+    for d in range(N):
+        n = d + 1
+        b = T.bb[:, d * K:(d + 1) * K]
+        l0 = d * LC
+        bsem, bcnt = (S.b0, 16) if d == 0 else (S["ab%d" % d], arrive[d])
+
+        for Q in (V, A):
+            Q.wait_ge(S.cv, ncv[0])
+            if d == 0:
+                Q.wait_ge(S.ref, 16)
+            else:
+                Q.wait_ge(S.sc, d)
+        for h in range(2):
+            c0 = l0 + 2 * h * KC
+            V.tensor_copy(T.rs[:, 2 * h * K:2 * (h + 1) * K],
+                          T.win[:].indirect(T.l16[:, c0:c0 + 2 * KC])).then_inc(S["vg%d" % h], 1)
+            c0 = l0 + (4 + 2 * h) * KC
+            A.activation(T.rs[:, (4 + 2 * h) * K:(6 + 2 * h) * K], T.win[:].indirect(T.l16[:, c0:c0 + 2 * KC]),
+                         fn.Copy).then_inc(S["sg%d" % h], 1)
+        for k in range(4):
+            V.wait_ge(S["pe%d" % k], n)
+            V.tensor_reduce(T.acc[:, k:k + 1], pw[k][:, 0:K], X, op.add,
+                            apply_absolute_value=True).then_inc(S.vr0 if k == 0 else S.vr, 1)
+            A.wait_ge(S["pe%d" % (4 + k)], n)
+            A.activation(T.junk[:, k * K:(k + 1) * K], pw[4 + k][:, 0:K], fn.Abs,
+                         accum_out=T.acc[:, 4 + k:5 + k]).then_inc(S.sa0 if k == 0 else S.sa, 1)
+        P.wait_ge(bsem, bcnt)
+        for k in (0, 4, 2, 6, 3, 7, 1, 5):
+            if k == 1 and d > 0:
+                P.wait_ge(S.cl, 2 * d)
+            P.matmul(pw[k][:, 0:K], T.idp[:], b, True, False)
+        for k in (0, 4, 1, 5, 6, 2, 7, 3):
+            if k % 2 == 0:
+                P.wait_ge(S[("vg%d" if k < 4 else "sg%d") % (k // 2 % 2)], n)
+            P.matmul(pw[k][:, 0:K], T.idn[:], T.rs[:, k * K:(k + 1) * K], False, True).then_inc(S["pe%d" % k], 1)
+        P.wait_ge(S.vr0, n)
+        P.matmul(pk1[:, 0:O], T.idp[:], T.cen[:], True, False)
+        P.matmul(pk1[:, 0:O], T.idp[:], T.ov[:], False, False)
+        P.wait_ge(S.sa0, n)
+        P.matmul(pk2[:, 0:O], T.idp[:], T.cen[:], True, False)
+
+        P.wait_ge(S.vr, 3 * n)
+        P.wait_ge(S.sa, 3 * n)
+        P.matmul(pk1[:, 0:O], T.g8[:], T.acc[:], False, True).then_inc(S.k1, 1)
+        P.matmul(pk2[:, 0:O], T.g8[:], T.acc[:], False, True).then_inc(S.k2, 1)
+        P.matmul(pta[:, 0:KA], T.idp[:], T.bb[:, d * K:d * K + KA], True, False)
+        P.matmul(ptb[:, 0:K - KA], T.idp[:], T.bb[:, d * K + KA:(d + 1) * K], True, False)
+        if 2 <= n < N:
+            V.wait_ge(S["al%d" % n], arrive[n])
+            convert(n)
+        V.wait_ge(S.k1, n)
+        V.tensor_reduce(T.mm[:, 0:1], pk1[:, 0:O], X, op.min).then_inc(S.m12, 1)
+        V.wait_ge(S.k2, n)
+        V.tensor_reduce(T.mm[:, 1:2], pk2[:, 0:O], X, op.min).then_inc(S.m12, 1)
+        V.wait_ge(S.m12, 2 * n)
+        V.tensor_scalar(T.w30[:], T.mm[:, 0:1], T.mm[:, 1:2], float(KC), op.subtract, op.mult).then_inc(S.t1, 1)
+        V.wait_ge(S.t1, n)
+        V.tensor_scalar(T.ofr[:], T.jr[:], T.w30[:], 16.0, op.add, op.mult).then_inc(S.t3, 1)
+        V.tensor_scalar(T.off[:], T.jc[:], T.w30[:], None, op.add).then_inc(S.t2, 1)
+
+        V.wait_ge(S.t3, n)
+        V.tensor_copy(T.rw[:, 0:KA], T.rs[:].indirect(T.ofr[:, 0:CA])).then_inc(S.ra, 1)
+        A.wait_ge(S.t3, n)
+        A.activation(T.rw[:, KA:K], T.rs[:].indirect(T.ofr[:, CA:KC]), fn.Copy).then_inc(S.rb, 1)
+        V.wait_ge(S.t2, n)
+        V.tensor_copy(T.lw[:], T.l32[:, l0:l0 + LC].indirect(T.off[:])).then_inc(S.lg, 1)
+        P.wait_ge(S.ra, n)
+        P.matmul(pta[:, 0:KA], T.idn[:], T.rw[:, 0:KA], False, True).then_inc(S.pa, 1)
+        P.wait_ge(S.rb, n)
+        P.matmul(ptb[:, 0:K - KA], T.idn[:], T.rw[:, KA:K], False, True).then_inc(S.pb, 1)
+        if n == 1:
+            V.wait_ge(S.al1, arrive[1])
+            convert(1)
+        V.wait_ge(S.pa, n)
+        V.tensor_scalar(T.cl[:, 0:KA], pta[:, 0:KA], -float(C), float(C), op.max, op.min).then_inc(S.cl, 1)
+        V.wait_ge(S.pb, n)
+        V.tensor_scalar(T.cl[:, KA:K], ptb[:, 0:K - KA], -float(C), float(C), op.max, op.min).then_inc(S.cl, 1)
+        V.wait_ge(S.lg, n)
+        V.wait_ge(S.cl, 2 * n)
+        V.tensor_tensor(T.win[:].indirect(T.lw[:, 0:KC]), T.rw[:], T.cl[:], op.add).then_inc(S.sc, 1)
+
+    Y.wait_ge(S.sc, N)
+    Y.dma_start(T.y[:], T.win[:]).then_inc(S.stored, 16)
+    Y.wait_ge(S.stored, 16)

@@ -1,15 +1,17 @@
 from concourse.mybir import AluOpType, AxisListType, ActivationFunctionType
 
 N, W, K, O, C = 4, 2048, 480, 8, 16
+G = 8
 KC = K // 16
 LC = O * KC
-CA = 12
-KA = 16 * CA
-CENTRE = -float(15 * 2 ** 20)
+VC = 124
+WV = (448, 416)
+CENTRE = -15 * 2 ** 20
 
 SCRATCH = {
     "win": ("sbuf", [128, W], "bfloat16"),
-    "l32": ("sbuf", [128, N * LC], "int32"),
+    "low": ("sbuf", [128, W], "float32"),
+    "l32": ("sbuf", [128, N * LC + 8], "int32"),
     "bb": ("sbuf", [128, N * K], "bfloat16"),
     "sl": ("sbuf", [128, (N - 1) * LC], "int32"),
     "sb": ("sbuf", [128, (N - 1) * K], "bfloat16"),
@@ -19,34 +21,35 @@ SCRATCH = {
     "acc": ("sbuf", [128, O], "float32"),
     "mm": ("sbuf", [128, 2], "float32"),
     "w30": ("sbuf", [128, 1], "float32"),
+    "jt": ("sbuf", [128, KC], "float32"),
+    "jr": ("sbuf", [128, KC], "float32"),
+    "jc": ("sbuf", [128, 2], "float32"),
     "off": ("sbuf", [128, 2], "uint16"),
     "ofr": ("sbuf", [128, KC], "uint16"),
     "lw": ("sbuf", [128, 32], "uint16"),
+    "bl": ("sbuf", [128, K], "float32"),
+    "top": ("sbuf", [128, K], "float32"),
+    "bot": ("sbuf", [128, K], "float32"),
     "rw": ("sbuf", [128, K], "bfloat16"),
+    "da": ("sbuf", [128, K], "bfloat16"),
     "cl": ("sbuf", [128, K], "bfloat16"),
-    "ones": ("sbuf", [128, 128], "bfloat16"),
-    "eights": ("sbuf", [128, 128], "float32"),
-    "gt": ("sbuf", [128, 128], "float32"),
-    "g8": ("sbuf", [128, 128], "float32"),
-    "idp": ("sbuf", [128, 128], "bfloat16"),
-    "idn": ("sbuf", [128, 128], "bfloat16"),
+    "pm": ("sbuf", [128, 256], "bfloat16"),
+    "ids": ("sbuf", [128, 256], "bfloat16"),
     "cen": ("sbuf", [128, O], "bfloat16"),
     "ov": ("sbuf", [128, O], "bfloat16"),
+    "e8": ("sbuf", [128, 128], "float32"),
+    "g8": ("sbuf", [128, 128], "float32"),
     "pi": ("sbuf", [128, 1], "int32"),
     "pq": ("sbuf", [128, 1], "int32"),
     "pf": ("sbuf", [128, 1], "float32"),
-    "jt": ("sbuf", [128, KC], "float32"),
-    "jc": ("sbuf", [128, 2], "float32"),
-    "jr": ("sbuf", [128, KC], "float32"),
 }
-for _k in range(O):
-    SCRATCH["pw%d" % _k] = ("psum", [128, 512], "float32")
+for _o in range(O):
+    SCRATCH["pw%d" % _o] = ("psum", [128, 512], "float32")
 SEMAPHORES = ["ref", "l0", "b0", "l1", "b1", "rest", "sent", "stored",
               "al1", "al2", "al3", "ab1", "ab2", "ab3",
-              "fill", "gio", "gid", "gg1", "gg2", "c1", "c2", "cst",
-              "cv", "sc", "vg0", "vg1", "sg0", "sg1", "pe0", "pe1", "pe2", "pe3", "pe4", "pe5", "pe6", "pe7",
-              "vr0", "vr", "sa0", "sa",
-              "k1", "k2", "m12", "t1", "t2", "t3", "lg", "ra", "rb", "pa", "pb", "cl"]
+              "fill", "fb", "bl0", "gp", "ge", "gid", "c1", "c2", "c4", "cst",
+              "cv", "sc", "vg0", "vg1", "sg0", "sg1", "vr0", "vr", "sa0", "sa", "mv", "bl",
+              "k1", "k2", "m12", "t1", "t2", "t3", "lg", "pv", "ps", "cl"] + ["pe%d" % _o for _o in range(O)]
 
 
 def rank_program(g, core, T, topo):
@@ -57,8 +60,9 @@ def rank_program(g, core, T, topo):
     V, A, P, Y = g.vector, g.scalar, g.tensor, g.sync
     op, fn = AluOpType, ActivationFunctionType
     X = AxisListType.X
-    pw = [T["pw%d" % k] for k in range(O)]
-    pk1, pk2, pta, ptb = pw[0], pw[4], pw[1], pw[5]
+    idp, idn = T.ids[:, 0:128], T.ids[:, 128:256]
+    pw = [T["pw%d" % o] for o in range(O)]
+    pk1, pk2 = pw[0], pw[6]
 
     Y.dma_start(T.l32[:, 0:LC], T.ops[:, rank * LC:(rank + 1) * LC]).then_inc(S.l0, 16)
     Y.dma_start(T.win[:], T.ref0[:]).then_inc(S.ref, 16)
@@ -68,29 +72,22 @@ def rank_program(g, core, T, topo):
         Y.dma_start(T.sl[:, (d - 1) * LC:d * LC], T.ops[:, q * LC:(q + 1) * LC]).then_inc(S.l1 if d == 1 else S.rest, 16)
         Y.dma_start(T.sb[:, (d - 1) * K:d * K], T.obs[:, q * K:(q + 1) * K]).then_inc(S.b1 if d == 1 else S.rest, 16)
 
-    V.memset(T.ones[:], 1.0).then_inc(S.fill, 1)
-    V.memset(T.eights[:], 8.0).then_inc(S.fill, 1)
-    V.memset(T.cen[:], CENTRE).then_inc(S.fill, 1)
-    g.iota(T.pi[:], [[0, 1]], 0, 1).then_inc(S.gio, 1)
-    g.iota(T.jt[:], [[16, KC]], 0, 1, allow_small_or_imprecise_dtypes=True).then_inc(S.gio, 1)
-    g.iota(T.ov[:], [[1, O]], 0, 0, allow_small_or_imprecise_dtypes=True).then_inc(S.gio, 1)
-    g.wait_ge(S.fill, 3)
-    g.affine_select(T.idp[:], T.ones[:], [[-1, 128]], op.is_equal, 0.0, 0, 1).then_inc(S.gid, 1)
-    g.affine_select(T.gt[:], T.eights[:], [[-16, 8], [0, 16]], op.is_ge, 0.0, 0, 1).then_inc(S.gg1, 1)
-    g.wait_ge(S.gg1, 1)
-    g.affine_select(T.g8[:], T.gt[:], [[16, 8], [0, 16]], op.is_ge, 0.0, 15, -1).then_inc(S.gg2, 1)
-    V.wait_ge(S.gio, 3)
-    V.tensor_scalar(T.pq[:], T.pi[:], 112, None, op.bitwise_and).then_inc(S.c1, 1)
-    V.wait_ge(S.c1, 1)
-    V.tensor_copy(T.pf[:], T.pq[:]).then_inc(S.c2, 1)
-    V.wait_ge(S.c2, 1)
-    V.tensor_scalar(T.jc[:], T.jt[:, 0:2], T.pf[:], float(KC - 1), op.subtract, op.min).then_inc(S.cst, 1)
-    V.tensor_scalar(T.jr[:], T.jt[:], T.pf[:], 1.0 / 16, op.subtract, op.mult).then_inc(S.cst, 1)
-    V.wait_ge(S.gid, 1)
-    V.tensor_scalar(T.idn[:], T.idp[:], -1.0, None, op.mult).then_inc(S.cst, 1)
-    V.wait_ge(S.cst, 3)
-    P.wait_ge(S.cst, 3)
-    P.wait_ge(S.gg2, 1)
+    V.memset(T.pm[:, 0:128], 1.0).then_inc(S.fill, 1)
+    V.memset(T.pm[:, 128:256], -1.0).then_inc(S.fill, 1)
+    V.memset(T.bl[:], -float(C)).then_inc(S.fb, 1)
+    small = dict(allow_small_or_imprecise_dtypes=True)
+    g.iota(T.pi[:], [[0, 1]], 0, 1).then_inc(S.gp, 1)
+    g.iota(T.jt[:], [[1, KC]], 0, 0, **small).then_inc(S.gp, 1)
+    g.iota(T.e8[:], [[0, 128]], 8, 0, **small).then_inc(S.ge, 1)
+    g.wait_ge(S.fill, 2)
+    g.affine_select(T.ids[:], T.pm[:], [[0, 2], [-1, 128]], op.is_equal, 0.0, 0, 1).then_inc(S.gid, 1)
+    g.wait_ge(S.ge, 1)
+    g.affine_select(T.e8[:], T.e8[:], [[-16, G], [0, 16]], op.is_ge, 0.0, 0, 1).then_inc(S.ge, 1)
+    g.iota(T.cen[:], [[0, O]], CENTRE, 0, **small).then_inc(S.cst, 1)
+    g.wait_ge(S.ge, 2)
+    g.affine_select(T.g8[:], T.e8[:], [[16, G], [0, 16]], op.is_ge, 0.0, 15, -1).then_inc(S.cst, 1)
+    g.iota(T.ov[:], [[1, O]], 0, 0, **small).then_inc(S.cst, 1)
+    g.iota(T.l32[:, N * LC:N * LC + 8], [[0, 8]], 0, 0).then_inc(S.c4, 1)
 
     sent = 0
     arrive = {}
@@ -108,97 +105,145 @@ def rank_program(g, core, T, topo):
         g.remote_dma(T.bb[:, d * K:(d + 1) * K], T.sb[:, (d - 1) * K:d * K], S["ab%d" % d], S.sent, pid, rid, m)
         sent += 2 * len(topo.engines(core, dst))
         arrive[d] = len(topo.engines(T.cores[(rank + d) % N], core))
+        if d == 1:
+            g.wait_ge(S.fb, 1)
+            g.dma_start(T.bl[:], T.obs[:, rank * K:(rank + 1) * K], accum_op=op.add).then_inc(S.bl0, 16)
     g.wait_ge(S.sent, sent)
 
-    ncv = [0]
-
     def convert(d):
+        if d > 0:
+            V.wait_ge(S["al%d" % d], arrive[d])
         V.tensor_copy(T.l16[:, d * LC:(d + 1) * LC], T.l32[:, d * LC:(d + 1) * LC]).then_inc(S.cv, 1)
-        ncv[0] += 1
 
+    def frame(d):
+        return (S.b0, 16) if d == 0 else (S["ab%d" % d], arrive[d])
+
+    V.wait_ge(S.gp, 2)
+    V.tensor_scalar(T.pq[:], T.pi[:], 15, None, op.bitwise_and).then_inc(S.c1, 1)
+    V.wait_ge(S.c1, 1)
+    V.tensor_scalar(T.pf[:], T.pq[:], 1.0 / 16, None, op.mult).then_inc(S.c2, 1)
     V.wait_ge(S.l0, 16)
     convert(0)
+    V.wait_ge(S.c2, 1)
+    V.tensor_scalar(T.jr[:], T.jt[:], T.pf[:], None, op.add).then_inc(S.c4, 1)
+    V.tensor_scalar(T.jc[:], T.jt[:, 0:2], T.pf[:], 16.0, op.add, op.mult).then_inc(S.c4, 1)
+    P.wait_ge(S.gid, 1)
 
     for d in range(N):
         n = d + 1
-        b = T.bb[:, d * K:(d + 1) * K]
-        l0 = d * LC
-        bsem, bcnt = (S.b0, 16) if d == 0 else (S["ab%d" % d], arrive[d])
+        last = n == N
+        b0, l0 = d * K, d * LC
+        b = T.bb[:, b0:b0 + K]
+        win = T.win if d == 0 else T.low
+        sign, shift = (-1.0 if last else 1.0), (0.0 if d == 0 else float(C))
+
+        def lists(c0, c1):
+            return win[:].indirect(T.l16[:, l0 + c0:l0 + c1])
 
         for Q in (V, A):
-            Q.wait_ge(S.cv, ncv[0])
+            Q.wait_ge(S.cv, n)
             if d == 0:
                 Q.wait_ge(S.ref, 16)
             else:
                 Q.wait_ge(S.sc, d)
-        for h in range(2):
-            c0 = l0 + 2 * h * KC
-            V.tensor_copy(T.rs[:, 2 * h * K:2 * (h + 1) * K],
-                          T.win[:].indirect(T.l16[:, c0:c0 + 2 * KC])).then_inc(S["vg%d" % h], 1)
-            c0 = l0 + (4 + 2 * h) * KC
-            A.activation(T.rs[:, (4 + 2 * h) * K:(6 + 2 * h) * K], T.win[:].indirect(T.l16[:, c0:c0 + 2 * KC]),
-                         fn.Copy).then_inc(S["sg%d" % h], 1)
-        for k in range(4):
-            V.wait_ge(S["pe%d" % k], n)
-            V.tensor_reduce(T.acc[:, k:k + 1], pw[k][:, 0:K], X, op.add,
+        for k, (c0, c1) in enumerate(((0, 2 * KC), (2 * KC, VC))):
+            if d == 0:
+                r = V.tensor_copy(T.rs[:, 16 * c0:16 * c1], lists(c0, c1))
+            else:
+                r = V.tensor_scalar(T.rs[:, 16 * c0:16 * c1], lists(c0, c1), shift, sign, op.add, op.mult)
+            r.then_inc(S["vg%d" % k], 1)
+        for k, (c0, c1) in enumerate(((6 * KC, LC), (VC, 6 * KC))):
+            A.activation(T.rs[:, 16 * c0:16 * c1], lists(c0, c1), fn.Copy, bias=sign * shift,
+                         scale=sign).then_inc(S["sg%d" % k], 1)
+        for k, (ov, os_) in enumerate(((0, 6), (1, 7), (2, 5), (3, 4))):
+            V.wait_ge(S["pe%d" % ov], n)
+            V.tensor_reduce(T.acc[:, ov:ov + 1], pw[ov][:, 0:K], X, op.add,
                             apply_absolute_value=True).then_inc(S.vr0 if k == 0 else S.vr, 1)
-            A.wait_ge(S["pe%d" % (4 + k)], n)
-            A.activation(T.junk[:, k * K:(k + 1) * K], pw[4 + k][:, 0:K], fn.Abs,
-                         accum_out=T.acc[:, 4 + k:5 + k]).then_inc(S.sa0 if k == 0 else S.sa, 1)
-        P.wait_ge(bsem, bcnt)
-        for k in (0, 4, 2, 6, 3, 7, 1, 5):
-            if k == 1 and d > 0:
-                P.wait_ge(S.cl, 2 * d)
-            P.matmul(pw[k][:, 0:K], T.idp[:], b, True, False)
-        for k in (0, 4, 1, 5, 6, 2, 7, 3):
-            if k % 2 == 0:
-                P.wait_ge(S[("vg%d" if k < 4 else "sg%d") % (k // 2 % 2)], n)
-            P.matmul(pw[k][:, 0:K], T.idn[:], T.rs[:, k * K:(k + 1) * K], False, True).then_inc(S["pe%d" % k], 1)
+            A.wait_ge(S["pe%d" % os_], n)
+            A.activation(T.junk[:, k * K:(k + 1) * K], pw[os_][:, 0:K], fn.Abs,
+                         accum_out=T.acc[:, os_:os_ + 1]).then_inc(S.sa0 if k == 0 else S.sa, 1)
+        P.wait_ge(*frame(d))
+        order = (0, 6, 7, 1, 5, 2, 4, 3)
+        ready = {0: S.vg0, 6: S.sg0, 5: S.sg1, 2: S.vg1}
+
+        def frame_in(ways):
+            for o in ways:
+                P.matmul(pw[o][:, 0:K], idp, b, True, False)
+
+        def values_off(ways):
+            for o in ways:
+                if o in ready:
+                    P.wait_ge(ready[o], n)
+                P.matmul(pw[o][:, 0:K], idp if last else idn, T.rs[:, o * K:(o + 1) * K], False,
+                         True).then_inc(S["pe%d" % o], 1)
+
+        if d == 0:
+            for half in (order[:4], order[4:]):
+                frame_in(half)
+                values_off(half)
+            P.wait_ge(S.cst, 3)
+        else:
+            frame_in(order[2:])
+            P.wait_ge(S.t1, d)
+            frame_in(order[:2])
+            values_off(order)
         P.wait_ge(S.vr0, n)
-        P.matmul(pk1[:, 0:O], T.idp[:], T.cen[:], True, False)
-        P.matmul(pk1[:, 0:O], T.idp[:], T.ov[:], False, False)
+        P.matmul(pk1[:, 0:O], idp, T.cen[:], True, False)
+        P.matmul(pk1[:, 0:O], idp, T.ov[:], False, False)
         P.wait_ge(S.sa0, n)
-        P.matmul(pk2[:, 0:O], T.idp[:], T.cen[:], True, False)
+        P.matmul(pk2[:, 0:O], idp, T.cen[:], True, False)
 
         P.wait_ge(S.vr, 3 * n)
         P.wait_ge(S.sa, 3 * n)
         P.matmul(pk1[:, 0:O], T.g8[:], T.acc[:], False, True).then_inc(S.k1, 1)
         P.matmul(pk2[:, 0:O], T.g8[:], T.acc[:], False, True).then_inc(S.k2, 1)
-        P.matmul(pta[:, 0:KA], T.idp[:], T.bb[:, d * K:d * K + KA], True, False)
-        P.matmul(ptb[:, 0:K - KA], T.idp[:], T.bb[:, d * K + KA:(d + 1) * K], True, False)
-        if 2 <= n < N:
-            V.wait_ge(S["al%d" % n], arrive[n])
+        if d == 0 or last:
+            src, dst, by = (T.win, T.low, -float(C)) if d == 0 else (T.low, T.win, float(C))
+            wv = WV[min(d, 1)]
+            V.tensor_scalar(dst[:, 0:wv], src[:, 0:wv], by, None, op.add).then_inc(S.mv, 1)
+            A.activation(dst[:, wv:W], src[:, wv:W], fn.Copy, bias=by).then_inc(S.mv, 1)
+        else:
+            A.activation(T.bl[:], b, fn.Copy, bias=-float(C)).then_inc(S.bl, 1)
             convert(n)
         V.wait_ge(S.k1, n)
         V.tensor_reduce(T.mm[:, 0:1], pk1[:, 0:O], X, op.min).then_inc(S.m12, 1)
         V.wait_ge(S.k2, n)
         V.tensor_reduce(T.mm[:, 1:2], pk2[:, 0:O], X, op.min).then_inc(S.m12, 1)
+        if d == 0:
+            V.wait_ge(S.c4, 3)
         V.wait_ge(S.m12, 2 * n)
         V.tensor_scalar(T.w30[:], T.mm[:, 0:1], T.mm[:, 1:2], float(KC), op.subtract, op.mult).then_inc(S.t1, 1)
         V.wait_ge(S.t1, n)
         V.tensor_scalar(T.ofr[:], T.jr[:], T.w30[:], 16.0, op.add, op.mult).then_inc(S.t3, 1)
         V.tensor_scalar(T.off[:], T.jc[:], T.w30[:], None, op.add).then_inc(S.t2, 1)
 
-        V.wait_ge(S.t3, n)
-        V.tensor_copy(T.rw[:, 0:KA], T.rs[:].indirect(T.ofr[:, 0:CA])).then_inc(S.ra, 1)
+        picked = T.rs[:].indirect(T.ofr[:])
         A.wait_ge(S.t3, n)
-        A.activation(T.rw[:, KA:K], T.rs[:].indirect(T.ofr[:, CA:KC]), fn.Copy).then_inc(S.rb, 1)
-        V.wait_ge(S.t2, n)
-        V.tensor_copy(T.lw[:], T.l32[:, l0:l0 + LC].indirect(T.off[:])).then_inc(S.lg, 1)
-        P.wait_ge(S.ra, n)
-        P.matmul(pta[:, 0:KA], T.idn[:], T.rw[:, 0:KA], False, True).then_inc(S.pa, 1)
-        P.wait_ge(S.rb, n)
-        P.matmul(ptb[:, 0:K - KA], T.idn[:], T.rw[:, KA:K], False, True).then_inc(S.pb, 1)
+        V.wait_ge(S.t3, n)
+        if last:
+            A.activation(T.rw[:], picked, fn.Copy, scale=-1.0).then_inc(S.ps, 1)
+            V.tensor_tensor(T.da[:], picked, b, op.add).then_inc(S.pv, 1)
+        else:
+            A.activation(T.bot[:], picked, fn.Copy, bias=-2.0 * C).then_inc(S.ps, 1)
+            V.wait_ge(*((S.bl0, 16) if d == 0 else (S.bl, d)))
+            V.tensor_tensor(T.top[:], picked, T.bl[:], op.min).then_inc(S.pv, 1)
         if n == 1:
-            V.wait_ge(S.al1, arrive[1])
             convert(1)
-        V.wait_ge(S.pa, n)
-        V.tensor_scalar(T.cl[:, 0:KA], pta[:, 0:KA], -float(C), float(C), op.max, op.min).then_inc(S.cl, 1)
-        V.wait_ge(S.pb, n)
-        V.tensor_scalar(T.cl[:, KA:K], ptb[:, 0:K - KA], -float(C), float(C), op.max, op.min).then_inc(S.cl, 1)
+        V.wait_ge(S.t2, n)
+        V.tensor_copy(T.lw[:], T.l32[:, l0:l0 + LC + 8].indirect(T.off[:])).then_inc(S.lg, 1)
+        if last:
+            V.wait_ge(S.pv, n)
+            V.tensor_scalar(T.cl[:], T.da[:], -float(C), float(C), op.max, op.min).then_inc(S.cl, 1)
+            V.wait_ge(S.cl, 1)
+        if d == 0 or last:
+            V.wait_ge(S.mv, 2 if d == 0 else 4)
         V.wait_ge(S.lg, n)
-        V.wait_ge(S.cl, 2 * n)
-        V.tensor_tensor(T.win[:].indirect(T.lw[:, 0:KC]), T.rw[:], T.cl[:], op.add).then_inc(S.sc, 1)
+        V.wait_ge(S.pv, n)
+        V.wait_ge(S.ps, n)
+        if last:
+            V.tensor_tensor(T.win[:].indirect(T.lw[:, 0:KC]), T.rw[:], T.cl[:], op.add).then_inc(S.sc, 1)
+        else:
+            V.tensor_tensor(T.low[:].indirect(T.lw[:, 0:KC]), T.top[:], T.bot[:], op.max).then_inc(S.sc, 1)
 
     Y.wait_ge(S.sc, N)
     Y.dma_start(T.y[:], T.win[:]).then_inc(S.stored, 16)

from concourse.mybir import AluOpType, AxisListType, ActivationFunctionType

N, W, K, O, C = 4, 2048, 480, 8, 16
G = 8
KC = K // 16
LC = O * KC
VC = 124
WV = (448, 416)
CENTRE = -15 * 2 ** 20

SCRATCH = {
    "win": ("sbuf", [128, W], "bfloat16"),
    "low": ("sbuf", [128, W], "float32"),
    "l32": ("sbuf", [128, N * LC + 8], "int32"),
    "bb": ("sbuf", [128, N * K], "bfloat16"),
    "sl": ("sbuf", [128, (N - 1) * LC], "int32"),
    "sb": ("sbuf", [128, (N - 1) * K], "bfloat16"),
    "l16": ("sbuf", [128, N * LC], "uint16"),
    "rs": ("sbuf", [128, O * K], "bfloat16"),
    "junk": ("sbuf", [128, 4 * K], "float32"),
    "acc": ("sbuf", [128, O], "float32"),
    "mm": ("sbuf", [128, 2], "float32"),
    "w30": ("sbuf", [128, 1], "float32"),
    "jt": ("sbuf", [128, KC], "float32"),
    "jr": ("sbuf", [128, KC], "float32"),
    "jc": ("sbuf", [128, 2], "float32"),
    "off": ("sbuf", [128, 2], "uint16"),
    "ofr": ("sbuf", [128, KC], "uint16"),
    "lw": ("sbuf", [128, 32], "uint16"),
    "bl": ("sbuf", [128, K], "float32"),
    "top": ("sbuf", [128, K], "float32"),
    "bot": ("sbuf", [128, K], "float32"),
    "rw": ("sbuf", [128, K], "bfloat16"),
    "da": ("sbuf", [128, K], "bfloat16"),
    "cl": ("sbuf", [128, K], "bfloat16"),
    "pm": ("sbuf", [128, 256], "bfloat16"),
    "ids": ("sbuf", [128, 256], "bfloat16"),
    "cen": ("sbuf", [128, O], "bfloat16"),
    "ov": ("sbuf", [128, O], "bfloat16"),
    "e8": ("sbuf", [128, 128], "float32"),
    "g8": ("sbuf", [128, 128], "float32"),
    "pi": ("sbuf", [128, 1], "int32"),
    "pq": ("sbuf", [128, 1], "int32"),
    "pf": ("sbuf", [128, 1], "float32"),
}
for _o in range(O):
    SCRATCH["pw%d" % _o] = ("psum", [128, 512], "float32")
SEMAPHORES = ["ref", "l0", "b0", "l1", "b1", "rest", "sent", "stored",
              "al1", "al2", "al3", "ab1", "ab2", "ab3",
              "fill", "fb", "bl0", "gp", "ge", "gid", "c1", "c2", "c4", "cst",
              "cv", "sc", "vg0", "vg1", "sg0", "sg1", "vr0", "vr", "sa0", "sa", "mv", "bl",
              "k1", "k2", "m12", "t1", "t2", "t3", "lg", "pv", "ps", "cl"] + ["pe%d" % _o for _o in range(O)]


def rank_program(g, core, T, topo):
    rank = T.rank_of(core)
    if rank is None:
        return
    S = T.sem
    V, A, P, Y = g.vector, g.scalar, g.tensor, g.sync
    op, fn = AluOpType, ActivationFunctionType
    X = AxisListType.X
    idp, idn = T.ids[:, 0:128], T.ids[:, 128:256]
    pw = [T["pw%d" % o] for o in range(O)]
    pk1, pk2 = pw[0], pw[6]

    Y.dma_start(T.l32[:, 0:LC], T.ops[:, rank * LC:(rank + 1) * LC]).then_inc(S.l0, 16)
    Y.dma_start(T.win[:], T.ref0[:]).then_inc(S.ref, 16)
    Y.dma_start(T.bb[:, 0:K], T.obs[:, rank * K:(rank + 1) * K]).then_inc(S.b0, 16)
    for d in range(1, N):
        q = (rank - d) % N
        Y.dma_start(T.sl[:, (d - 1) * LC:d * LC], T.ops[:, q * LC:(q + 1) * LC]).then_inc(S.l1 if d == 1 else S.rest, 16)
        Y.dma_start(T.sb[:, (d - 1) * K:d * K], T.obs[:, q * K:(q + 1) * K]).then_inc(S.b1 if d == 1 else S.rest, 16)

    V.memset(T.pm[:, 0:128], 1.0).then_inc(S.fill, 1)
    V.memset(T.pm[:, 128:256], -1.0).then_inc(S.fill, 1)
    V.memset(T.bl[:], -float(C)).then_inc(S.fb, 1)
    small = dict(allow_small_or_imprecise_dtypes=True)
    g.iota(T.pi[:], [[0, 1]], 0, 1).then_inc(S.gp, 1)
    g.iota(T.jt[:], [[1, KC]], 0, 0, **small).then_inc(S.gp, 1)
    g.iota(T.e8[:], [[0, 128]], 8, 0, **small).then_inc(S.ge, 1)
    g.wait_ge(S.fill, 2)
    g.affine_select(T.ids[:], T.pm[:], [[0, 2], [-1, 128]], op.is_equal, 0.0, 0, 1).then_inc(S.gid, 1)
    g.wait_ge(S.ge, 1)
    g.affine_select(T.e8[:], T.e8[:], [[-16, G], [0, 16]], op.is_ge, 0.0, 0, 1).then_inc(S.ge, 1)
    g.iota(T.cen[:], [[0, O]], CENTRE, 0, **small).then_inc(S.cst, 1)
    g.wait_ge(S.ge, 2)
    g.affine_select(T.g8[:], T.e8[:], [[16, G], [0, 16]], op.is_ge, 0.0, 15, -1).then_inc(S.cst, 1)
    g.iota(T.ov[:], [[1, O]], 0, 0, **small).then_inc(S.cst, 1)
    g.iota(T.l32[:, N * LC:N * LC + 8], [[0, 8]], 0, 0).then_inc(S.c4, 1)

    sent = 0
    arrive = {}
    for d in range(1, N):
        dst = T.cores[(rank - d) % N]
        rid, pid = topo.addr(dst, core)
        m = topo.mask(core, dst)
        if d == 1:
            g.wait_ge(S.l1, 16)
        if d == 2:
            g.wait_ge(S.rest, 16 * 2 * (N - 2))
        g.remote_dma(T.l32[:, d * LC:(d + 1) * LC], T.sl[:, (d - 1) * LC:d * LC], S["al%d" % d], S.sent, pid, rid, m)
        if d == 1:
            g.wait_ge(S.b1, 16)
        g.remote_dma(T.bb[:, d * K:(d + 1) * K], T.sb[:, (d - 1) * K:d * K], S["ab%d" % d], S.sent, pid, rid, m)
        sent += 2 * len(topo.engines(core, dst))
        arrive[d] = len(topo.engines(T.cores[(rank + d) % N], core))
        if d == 1:
            g.wait_ge(S.fb, 1)
            g.dma_start(T.bl[:], T.obs[:, rank * K:(rank + 1) * K], accum_op=op.add).then_inc(S.bl0, 16)
    g.wait_ge(S.sent, sent)

    def convert(d):
        if d > 0:
            V.wait_ge(S["al%d" % d], arrive[d])
        V.tensor_copy(T.l16[:, d * LC:(d + 1) * LC], T.l32[:, d * LC:(d + 1) * LC]).then_inc(S.cv, 1)

    def frame(d):
        return (S.b0, 16) if d == 0 else (S["ab%d" % d], arrive[d])

    V.wait_ge(S.gp, 2)
    V.tensor_scalar(T.pq[:], T.pi[:], 15, None, op.bitwise_and).then_inc(S.c1, 1)
    V.wait_ge(S.c1, 1)
    V.tensor_scalar(T.pf[:], T.pq[:], 1.0 / 16, None, op.mult).then_inc(S.c2, 1)
    V.wait_ge(S.l0, 16)
    convert(0)
    V.wait_ge(S.c2, 1)
    V.tensor_scalar(T.jr[:], T.jt[:], T.pf[:], None, op.add).then_inc(S.c4, 1)
    V.tensor_scalar(T.jc[:], T.jt[:, 0:2], T.pf[:], 16.0, op.add, op.mult).then_inc(S.c4, 1)
    P.wait_ge(S.gid, 1)

    for d in range(N):
        n = d + 1
        last = n == N
        b0, l0 = d * K, d * LC
        b = T.bb[:, b0:b0 + K]
        win = T.win if d == 0 else T.low
        sign, shift = (-1.0 if last else 1.0), (0.0 if d == 0 else float(C))

        def lists(c0, c1):
            return win[:].indirect(T.l16[:, l0 + c0:l0 + c1])

        for Q in (V, A):
            Q.wait_ge(S.cv, n)
            if d == 0:
                Q.wait_ge(S.ref, 16)
            else:
                Q.wait_ge(S.sc, d)
        for k, (c0, c1) in enumerate(((0, 2 * KC), (2 * KC, VC))):
            if d == 0:
                r = V.tensor_copy(T.rs[:, 16 * c0:16 * c1], lists(c0, c1))
            else:
                r = V.tensor_scalar(T.rs[:, 16 * c0:16 * c1], lists(c0, c1), shift, sign, op.add, op.mult)
            r.then_inc(S["vg%d" % k], 1)
        for k, (c0, c1) in enumerate(((6 * KC, LC), (VC, 6 * KC))):
            A.activation(T.rs[:, 16 * c0:16 * c1], lists(c0, c1), fn.Copy, bias=sign * shift,
                         scale=sign).then_inc(S["sg%d" % k], 1)
        for k, (ov, os_) in enumerate(((0, 6), (1, 7), (2, 5), (3, 4))):
            V.wait_ge(S["pe%d" % ov], n)
            V.tensor_reduce(T.acc[:, ov:ov + 1], pw[ov][:, 0:K], X, op.add,
                            apply_absolute_value=True).then_inc(S.vr0 if k == 0 else S.vr, 1)
            A.wait_ge(S["pe%d" % os_], n)
            A.activation(T.junk[:, k * K:(k + 1) * K], pw[os_][:, 0:K], fn.Abs,
                         accum_out=T.acc[:, os_:os_ + 1]).then_inc(S.sa0 if k == 0 else S.sa, 1)
        P.wait_ge(*frame(d))
        order = (0, 6, 7, 1, 5, 2, 4, 3)
        ready = {0: S.vg0, 6: S.sg0, 5: S.sg1, 2: S.vg1}

        def frame_in(ways):
            for o in ways:
                P.matmul(pw[o][:, 0:K], idp, b, True, False)

        def values_off(ways):
            for o in ways:
                if o in ready:
                    P.wait_ge(ready[o], n)
                P.matmul(pw[o][:, 0:K], idp if last else idn, T.rs[:, o * K:(o + 1) * K], False,
                         True).then_inc(S["pe%d" % o], 1)

        if d == 0:
            for half in (order[:4], order[4:]):
                frame_in(half)
                values_off(half)
            P.wait_ge(S.cst, 3)
        else:
            frame_in(order[2:])
            P.wait_ge(S.t1, d)
            frame_in(order[:2])
            values_off(order)
        P.wait_ge(S.vr0, n)
        P.matmul(pk1[:, 0:O], idp, T.cen[:], True, False)
        P.matmul(pk1[:, 0:O], idp, T.ov[:], False, False)
        P.wait_ge(S.sa0, n)
        P.matmul(pk2[:, 0:O], idp, T.cen[:], True, False)

        P.wait_ge(S.vr, 3 * n)
        P.wait_ge(S.sa, 3 * n)
        P.matmul(pk1[:, 0:O], T.g8[:], T.acc[:], False, True).then_inc(S.k1, 1)
        P.matmul(pk2[:, 0:O], T.g8[:], T.acc[:], False, True).then_inc(S.k2, 1)
        if d == 0 or last:
            src, dst, by = (T.win, T.low, -float(C)) if d == 0 else (T.low, T.win, float(C))
            wv = WV[min(d, 1)]
            V.tensor_scalar(dst[:, 0:wv], src[:, 0:wv], by, None, op.add).then_inc(S.mv, 1)
            A.activation(dst[:, wv:W], src[:, wv:W], fn.Copy, bias=by).then_inc(S.mv, 1)
        else:
            A.activation(T.bl[:], b, fn.Copy, bias=-float(C)).then_inc(S.bl, 1)
            convert(n)
        V.wait_ge(S.k1, n)
        V.tensor_reduce(T.mm[:, 0:1], pk1[:, 0:O], X, op.min).then_inc(S.m12, 1)
        V.wait_ge(S.k2, n)
        V.tensor_reduce(T.mm[:, 1:2], pk2[:, 0:O], X, op.min).then_inc(S.m12, 1)
        if d == 0:
            V.wait_ge(S.c4, 3)
        V.wait_ge(S.m12, 2 * n)
        V.tensor_scalar(T.w30[:], T.mm[:, 0:1], T.mm[:, 1:2], float(KC), op.subtract, op.mult).then_inc(S.t1, 1)
        V.wait_ge(S.t1, n)
        V.tensor_scalar(T.ofr[:], T.jr[:], T.w30[:], 16.0, op.add, op.mult).then_inc(S.t3, 1)
        V.tensor_scalar(T.off[:], T.jc[:], T.w30[:], None, op.add).then_inc(S.t2, 1)

        picked = T.rs[:].indirect(T.ofr[:])
        A.wait_ge(S.t3, n)
        V.wait_ge(S.t3, n)
        if last:
            A.activation(T.rw[:], picked, fn.Copy, scale=-1.0).then_inc(S.ps, 1)
            V.tensor_tensor(T.da[:], picked, b, op.add).then_inc(S.pv, 1)
        else:
            A.activation(T.bot[:], picked, fn.Copy, bias=-2.0 * C).then_inc(S.ps, 1)
            V.wait_ge(*((S.bl0, 16) if d == 0 else (S.bl, d)))
            V.tensor_tensor(T.top[:], picked, T.bl[:], op.min).then_inc(S.pv, 1)
        if n == 1:
            convert(1)
        V.wait_ge(S.t2, n)
        V.tensor_copy(T.lw[:], T.l32[:, l0:l0 + LC + 8].indirect(T.off[:])).then_inc(S.lg, 1)
        if last:
            V.wait_ge(S.pv, n)
            V.tensor_scalar(T.cl[:], T.da[:], -float(C), float(C), op.max, op.min).then_inc(S.cl, 1)
            V.wait_ge(S.cl, 1)
        if d == 0 or last:
            V.wait_ge(S.mv, 2 if d == 0 else 4)
        V.wait_ge(S.lg, n)
        V.wait_ge(S.pv, n)
        V.wait_ge(S.ps, n)
        if last:
            V.tensor_tensor(T.win[:].indirect(T.lw[:, 0:KC]), T.rw[:], T.cl[:], op.add).then_inc(S.sc, 1)
        else:
            V.tensor_tensor(T.low[:].indirect(T.lw[:, 0:KC]), T.top[:], T.bot[:], op.max).then_inc(S.sc, 1)

    Y.wait_ge(S.sc, N)
    Y.dma_start(T.y[:], T.win[:]).then_inc(S.stored, 16)
    Y.wait_ge(S.stored, 16)
